import numpy as np
import ml_dtypes


def mxq(x, axis, fmt="e4m3"):
    dtype, down = {"e4m3": (ml_dtypes.float8_e4m3fn, 7), "e5m2": (ml_dtypes.float8_e5m2, 14)}[fmt]
    v = np.moveaxis(np.asarray(x, np.float32).astype(ml_dtypes.bfloat16).astype(np.float64), axis, -1)
    blocks = v.reshape(v.shape[:-1] + (-1, 32))
    amax = np.abs(blocks).max(-1, keepdims=True)
    byte = np.maximum(np.where(amax > 0, np.frexp(amax)[1] - 1 + 127, 0) - down, 1)
    scale = np.exp2(byte - 127.0)
    codes = (blocks / scale).astype(np.float32).astype(dtype).astype(np.float64)
    return np.moveaxis((codes * scale).reshape(v.shape), -1, axis)


WIDE = False


def mx_kscale(k):
    if not WIDE:
        return np.ones(k)
    levels = np.array([10, -10, 5, -5, 0])
    if k % 512:
        return np.exp2(np.random.permutation(np.resize(levels, k // 32))).repeat(32)
    a = np.empty((k // 512, 16))
    for p in range(k // 512):
        a[p, :8] = np.random.permutation(np.resize(levels, 8))
        for g in range(8):
            far = levels[np.abs(levels - a[p, g]) >= 10]
            a[p, g + 8] = far[np.random.randint(len(far))]
    return np.exp2(a.ravel()).repeat(32)


def f64(x):
    return np.asarray(x).astype(np.float64)


def striped(idx):
    return np.tile(np.asarray(idx).reshape(-1, 16).T, (8, 1)).astype(np.uint16)


def unstriped(offs):
    return offs[:16].T.reshape(-1).astype(np.int64)


E2M1 = np.array([0.0, 0.5, 1.0, 1.5, 2.0, 3.0, 4.0, 6.0, -0.0, -0.5, -1.0, -1.5, -2.0, -3.0, -4.0, -6.0])


def pack_weight(w, fmt):
    k, n = w.shape
    w = f64(np.asarray(w, np.float32).astype(ml_dtypes.bfloat16)).reshape(k // 32, 32, n)
    amax = np.abs(w).max(1)
    if fmt == "e4m3":
        byte = np.frexp(amax)[1] - 1 + 127 - 7
    else:
        mant, ex = np.frexp(amax / 6.0)
        byte = np.where(mant > 0.5, ex, ex - 1) + 127
    byte = np.clip(np.where(amax > 0, byte, 1), 1, 254)
    scaled = (w * np.exp2(127.0 - byte)[:, None, :]).reshape(k, n).astype(np.float32)
    by_word = np.ascontiguousarray(scaled.reshape(k // 512, 128, 4, n).transpose(0, 1, 3, 2))
    if fmt == "e4m3":
        words = by_word.astype(ml_dtypes.float8_e4m3fn).view(np.uint8)
    else:
        c = by_word.astype(ml_dtypes.float4_e2m1fn).view(np.uint8) & 0xF
        words = (c[..., 0::2] | (c[..., 1::2] << 4)).reshape(k // 512, 128, 2 * n)
    return np.ascontiguousarray(words), np.ascontiguousarray(byte.astype(np.uint8).reshape(k // 512, 16, n))


def unpack_weight(words, scales, fmt):
    g, _, n = scales.shape
    words = np.ascontiguousarray(words).reshape(g, 128, n, -1)
    if fmt == "e4m3":
        vals = words.view(ml_dtypes.float8_e4m3fn).astype(np.float64)
    else:
        nib = np.empty((g, 128, n, 4), np.uint8)
        nib[..., 0::2] = words & 0xF
        nib[..., 1::2] = words >> 4
        vals = E2M1[nib]
    vals = vals * np.repeat(np.exp2(scales.astype(np.float64) - 127.0), 8, axis=1)[..., None]
    return vals.transpose(0, 1, 3, 2).reshape(g * 512, n)


def bf(x):
    return np.asarray(x, np.float32).astype(ml_dtypes.bfloat16)


def planes(Y):
    r, m = Y.shape
    b = f64(bf(Y)).reshape(r // 32, 32, m)
    amax = np.abs(b).max(1)
    byte = np.clip(np.where(amax > 0, np.frexp(amax)[1] - 1 + 127 - 7, 1), 1, 254)
    codes = (b * np.exp2(127.0 - byte)[:, None, :]).reshape(r, m).astype(np.float32).astype(ml_dtypes.float8_e4m3fn).view(np.uint8)
    words = codes.reshape(r // 512, 128, 4, m).transpose(0, 1, 3, 2)
    return np.ascontiguousarray(words), np.ascontiguousarray(byte.astype(np.uint8).reshape(r // 512, 16, m))


D, T, I, Q, E, Z, M, C = 512, 2048, 512, 256, 512, 1024, 1024, 512


def setup_inputs():
    n = np.random.standard_normal
    idx = np.random.permutation(T)[:I]
    idx2 = np.random.permutation(Z)[:I]
    idx3 = np.random.permutation(M)[:Q]
    fd = mx_kscale(D)
    fi = mx_kscale(I)
    fc = mx_kscale(C)
    ti = np.ones(T)
    ti[idx] = fi
    keysp = pack_weight(n((D, T)) / fd[:, None], "e2m1")
    return {
        "query": (n((D, Q)) * 1.0 / np.sqrt(D) * fd[:, None]).astype(np.float32),
        "keys_words": keysp[0],
        "keys_scales": keysp[1],
        "earl": (np.random.uniform(0.3, 1.7, (Q, Z))).astype(np.float32),
        "os": (np.random.uniform(0.02, 0.08, (1, I)) * fi).astype(np.float32),
        "vals": (n((E, T)) / ti).astype(np.float32),
        "wm": (n((C, E)) * 1.0 / np.sqrt(C) * fc[:, None]).astype(np.float32),
        "mstore": (n((C, M)) / fc[:, None]).astype(np.float32),
        "offs": striped(idx),
        "offs2": striped(idx2),
        "offs3": striped(idx3),
    }


def reference(query, keys_words, keys_scales, earl, os, vals, wm, mstore, offs, offs2, offs3):
    idx = unstriped(offs)
    idx2 = unstriped(offs2)
    idx3 = unstriped(offs3)
    keysu = unpack_weight(keys_words, keys_scales, "e2m1")
    queryq = mxq(f64(query), 0, "e4m3")
    keysidxg = keysu[:, idx]
    a = queryq.T @ keysidxg
    w = a * f64(earl)[:, idx2]
    wo1 = w * f64(os)
    wt1 = wo1.T
    vt1 = f64(vals)[:, idx].T
    vt1q = mxq(vt1, 0, "e4m3")
    wt1q = mxq(wt1, 0, "e4m3")
    o = vt1q.T @ wt1q
    wmq = mxq(f64(wm), 0, "e4m3")
    mstoreq = mxq(f64(mstore), 0, "e4m3")
    me = wmq.T @ mstoreq
    y = o * me[:, idx3]
    words, scales = planes(y)
    return y, words, scales

@@ -1,0 +1,188 @@
+from contextlib import ExitStack
+
+import concourse.mybir as mybir
+from concourse.masks import make_identity
+
+D, T, I, Q, E, Z, M, C = 512, 2048, 512, 256, 512, 1024, 1024, 512
+FLOPS = 2 * (D * Q * I + I * E * Q + C * E * M)
+
+F32 = mybir.dt.float32
+BF16 = mybir.dt.bfloat16
+I32 = mybir.dt.int32
+U32 = mybir.dt.uint32
+U16 = mybir.dt.uint16
+U8 = mybir.dt.uint8
+FP8X4 = mybir.dt.float8_e4m3fn_x4
+FP4X4 = mybir.dt.float4_e2m1fn_x4
+MULT = mybir.AluOpType.mult
+COPY = mybir.ActivationFunctionType.Copy
+
+P = 128
+PACK = 4
+BANK = 512
+
+
+def tile_attend_earliertable_remembered_lean_pl_kernel(
+    tc, query, keys_words, keys_scales, earl, slot_factor, vals, wm, mstore, offs, offs2, offs3,
+    out_0, out_1, out_2,
+):
+    nc = tc.nc
+    with ExitStack() as ctx:
+        sb = ctx.enter_context(tc.tile_pool(name="sb", bufs=1))
+        mm = ctx.enter_context(tc.psum_pool(name="mm", bufs=4))
+        tr = ctx.enter_context(tc.psum_pool(name="tr", bufs=4))
+
+        def quantise(name, grouped, width):
+            codes = sb.tile([P, width], U32, name=name + "_codes", align_bytes=64)
+            scales = sb.tile([P, width], U8, name=name + "_scales", align_bytes=64)
+            nc.vector.quantize_mx(out=codes[:].bitcast(FP8X4), scales=scales[:], in_=grouped)
+            return codes, scales
+
+        def interleave(engine_copy, dst, src):
+            engine_copy(
+                out=dst.rearrange("p (c i) t -> p c t i", i=4),
+                in_=src.rearrange("p t (c i) -> p c t i", i=4),
+            )
+
+        idx = sb.tile([P, I // 16], U16, name="idx")
+        idx2 = sb.tile([P, I // 16], U16, name="idx2")
+        idx3 = sb.tile([P, Q // 16], U16, name="idx3")
+        wm_raw = sb.tile([P, PACK, E], F32, name="wm_raw")
+        ms_raw = [sb.tile([P, PACK, BANK], F32, name=f"ms_raw{h}") for h in range(2)]
+        q_raw = sb.tile([P, PACK, Q], F32, name="q_raw")
+        key_pool = sb.tile([P, T], U16, name="key_pool")
+        key_pool_scales = sb.tile([P, T], U8, name="key_pool_scales")
+        earl_rows = [sb.tile([P, Z], F32, name=f"earl_rows{h}") for h in range(2)]
+        val_rows = [sb.tile([P, T], F32, name=f"val_rows{t}") for t in range(PACK)]
+        factor = sb.tile([P, 1, PACK], F32, name="factor")
+        ident = sb.tile([P, P], F32, name="ident")
+
+        nc.vector.memset(key_pool_scales[:].bitcast(I32), 0)
+        make_identity(nc, ident[:])
+
+        ms_view = mstore.rearrange("(p j) m -> p j m", j=PACK)
+        vals_view = vals.rearrange("(p t) c -> t p c", t=PACK)
+
+        def load_key_scales(g):
+            nc.sync.dma_start(
+                out=key_pool_scales[32 * g : 32 * g + 4, :].bitcast(I32),
+                in_=keys_scales[0, 4 * g : 4 * g + 4, :].bitcast(I32),
+            )
+
+        nc.sync.dma_start(out=wm_raw[:], in_=wm.rearrange("(p j) e -> p j e", j=PACK))
+        nc.sync.dma_start(out=ms_raw[0][:], in_=ms_view[:, :, 0:BANK])
+        nc.sync.dma_start(idx[:], offs)
+        nc.sync.dma_start(out=ms_raw[1][:], in_=ms_view[:, :, BANK : 2 * BANK])
+        load_key_scales(0)
+        load_key_scales(1)
+        nc.sync.dma_start(out=q_raw[:], in_=query.rearrange("(p j) q -> p j q", j=PACK))
+        load_key_scales(2)
+        load_key_scales(3)
+        nc.sync.dma_start(out=key_pool[:].bitcast(I32), in_=keys_words[0].bitcast(I32))
+        nc.sync.dma_start(idx2[:], offs2)
+        nc.sync.dma_start(out=earl_rows[0][:], in_=earl[0:P, :])
+        nc.sync.dma_start(out=factor[:], in_=slot_factor.rearrange("o (p t) -> p o t", t=PACK))
+        nc.sync.dma_start(out=earl_rows[1][:], in_=earl[P : 2 * P, :])
+        nc.sync.dma_start(idx3[:], offs3)
+        for t in range(PACK):
+            nc.sync.dma_start(out=val_rows[t][:], in_=vals_view[t])
+
+        wm_bf = sb.tile([P, PACK * E], BF16, name="wm_bf", align_bytes=64)
+        nc.vector.tensor_copy(
+            out=wm_bf[:].rearrange("p (t m j) -> p m j t", t=PACK, j=PACK),
+            in_=wm_raw[:].rearrange("p j (m t) -> p m j t", t=PACK),
+        )
+        wm_codes, wm_scales = quantise("wm", wm_bf[:], E)
+        me = [sb.tile([P, M], F32, name=f"me{t}") for t in range(PACK)]
+        for h in range(2):
+            ms_bf = sb.tile([P, BANK, PACK], BF16, name=f"ms_bf{h}", align_bytes=64)
+            interleave(nc.vector.tensor_copy, ms_bf[:], ms_raw[h][:])
+            ms_codes, ms_scales = quantise(f"ms{h}", ms_bf[:].rearrange("p c t -> p (c t)"), BANK)
+            for t in range(PACK):
+                cols = slice(t * P, (t + 1) * P)
+                acc = mm.tile([P, BANK], F32, name="acc")
+                nc.tensor.matmul_mx(
+                    out=acc[:], lhsT=wm_codes[:, cols].bitcast(FP8X4), lhsT_scale=wm_scales[:, cols],
+                    rhs=ms_codes[:].bitcast(FP8X4), rhs_scale=ms_scales[:], start=True, stop=True,
+                )
+                nc.scalar.copy(out=me[t][:, h * BANK : (h + 1) * BANK], in_=acc[:])
+
+        q_bf = sb.tile([P, Q, PACK], BF16, name="q_bf", align_bytes=64)
+        interleave(nc.vector.tensor_copy, q_bf[:], q_raw[:])
+        q_codes, q_scales = quantise("q", q_bf[:].rearrange("p c t -> p (c t)"), Q)
+        keys = sb.tile([P, I], U16, name="keys", align_bytes=64)
+        key_scales = sb.tile([P, I], U8, name="key_scales", align_bytes=64)
+        nc.vector.tensor_copy(out=keys[:], in_=key_pool[:].indirect(idx[:]))
+        nc.vector.tensor_copy(out=key_scales[:], in_=key_pool_scales[:].indirect(idx[:]))
+        w_bf = sb.tile([P, Q, PACK], BF16, name="w_bf", align_bytes=64)
+        for h in range(2):
+            rows = slice(h * P, (h + 1) * P)
+            earl_g = sb.tile([P, I], F32, name=f"earl_g{h}")
+            nc.scalar.activation(out=earl_g[:], in_=earl_rows[h][:].indirect(idx2[:]), func=COPY)
+            acc = mm.tile([P, BANK], F32, name="acc")
+            nc.tensor.matmul_mx(
+                out=acc[:], lhsT=q_codes[:, rows].bitcast(FP8X4), lhsT_scale=q_scales[:, rows],
+                rhs=keys[:].bitcast(FP4X4), rhs_scale=key_scales[:], start=True, stop=True,
+            )
+            w = sb.tile([P, I], F32, name=f"w{h}")
+            nc.vector.tensor_tensor(out=w[:], in0=acc[:], in1=earl_g[:], op=MULT)
+            turned = tr.tile([P, PACK, P], F32, name="turned")
+            for t in range(PACK):
+                nc.tensor.transpose(turned[:, t, :], w[:, t:I:PACK], ident[:])
+            nc.vector.tensor_tensor(
+                out=w_bf[:, rows, :], in0=turned[:].rearrange("p t q -> p q t"),
+                in1=factor[:].to_broadcast([P, P, PACK]), op=MULT,
+            )
+        w_codes, w_scales = quantise("w", w_bf[:].rearrange("p c t -> p (c t)"), Q)
+
+        me_g = []
+        for t in range(PACK):
+            picked = sb.tile([P, Q], F32, name=f"me_g{t}")
+            nc.vector.tensor_copy(out=picked[:], in_=me[t][:].indirect(idx3[:]))
+            me_g.append(picked)
+
+        y = sb.tile([P, PACK, Q], F32, name="y")
+        out_rows = out_0.rearrange("(p t) q -> p t q", t=PACK)
+        for t in range(PACK):
+            val_g = sb.tile([P, I], BF16, name=f"val_g{t}")
+            if t < PACK - 1:
+                nc.scalar.activation(out=val_g[:], in_=val_rows[t][:].indirect(idx[:]), func=COPY)
+            else:
+                nc.vector.tensor_copy(out=val_g[:, 0 : I // 2], in_=val_rows[t][:].indirect(idx[:, 0:16]))
+                nc.scalar.activation(
+                    out=val_g[:, I // 2 : I], in_=val_rows[t][:].indirect(idx[:, 16:32]), func=COPY
+                )
+            words = val_g[:].bitcast(F32)
+            turned = tr.tile([P, 2, P], F32, name="turned")
+            for u in range(2):
+                nc.tensor.transpose(turned[:, u, :], words[:, u : I // 2 : 2], ident[:])
+            v_bf = sb.tile([P, P * PACK], BF16, name=f"v_bf{t}", align_bytes=64)
+            nc.vector.tensor_copy(
+                out=v_bf[:].bitcast(F32).rearrange("p (e u) -> p e u", u=2),
+                in_=turned[:].rearrange("p u e -> p e u"),
+            )
+            v_codes, v_scales = quantise(f"v{t}", v_bf[:], P)
+            acc = mm.tile([P, Q], F32, name="acc")
+            nc.tensor.matmul_mx(
+                out=acc[:], lhsT=v_codes[:].bitcast(FP8X4), lhsT_scale=v_scales[:],
+                rhs=w_codes[:].bitcast(FP8X4), rhs_scale=w_scales[:], start=True, stop=True,
+            )
+            nc.vector.tensor_tensor(out=y[:, t, :], in0=acc[:], in1=me_g[t][:], op=MULT)
+            if t == PACK - 2:
+                nc.sync.dma_start(out=out_rows[:, 0 : PACK - 1, :], in_=y[:, 0 : PACK - 1, :])
+        nc.sync.dma_start(out=out_rows[:, PACK - 1, :], in_=y[:, PACK - 1, :])
+
+        y_bf = sb.tile([P, Q, PACK], BF16, name="y_bf", align_bytes=64)
+        split = 160
+        interleave(nc.vector.tensor_copy, y_bf[:, 0:split, :], y[:, :, 0:split])
+        interleave(nc.scalar.copy, y_bf[:, split:Q, :], y[:, :, split:Q])
+        y_codes, y_scales = quantise("y", y_bf[:].rearrange("p c t -> p (c t)"), Q)
+        nc.sync.dma_start(
+            out=out_1[0].rearrange("p c r -> p (c r)").bitcast(I32), in_=y_codes[:].bitcast(I32)
+        )
+        for g in range(4):
+            queue = nc.scalar if g % 2 == 0 else nc.sync
+            queue.dma_start(
+                out=out_2[0, 4 * g : 4 * g + 4, :].bitcast(I32),
+                in_=y_scales[32 * g : 32 * g + 4, :].bitcast(I32),
+            )

@@ -30,7 +30,8 @@ def tile_attend_earliertable_remembered_lean_pl_kernel(
     with ExitStack() as ctx:
         sb = ctx.enter_context(tc.tile_pool(name="sb", bufs=1))
         mm = ctx.enter_context(tc.psum_pool(name="mm", bufs=4))
-        tr = ctx.enter_context(tc.psum_pool(name="tr", bufs=4))
+        sc = ctx.enter_context(tc.psum_pool(name="sc", bufs=2))
+        tr = ctx.enter_context(tc.psum_pool(name="tr", bufs=2))
 
         def quantise(name, grouped, width):
             codes = sb.tile([P, width], U32, name=name + "_codes", align_bytes=64)
@@ -53,51 +54,85 @@ def tile_attend_earliertable_remembered_lean_pl_kernel(
         key_pool = sb.tile([P, T], U16, name="key_pool")
         key_pool_scales = sb.tile([P, T], U8, name="key_pool_scales")
         earl_rows = [sb.tile([P, Z], F32, name=f"earl_rows{h}") for h in range(2)]
-        val_rows = [sb.tile([P, T], F32, name=f"val_rows{t}") for t in range(PACK)]
+        val_rows = [sb.tile([P, T], F32, name=f"val_rows{t}", tag=f"val_rows{t}", align_bytes=64) for t in range(PACK)]
         factor = sb.tile([P, 1, PACK], F32, name="factor")
         ident = sb.tile([P, P], F32, name="ident")
 
-        nc.vector.memset(key_pool_scales[:].bitcast(I32), 0)
+        nc.gpsimd.memset(key_pool_scales[:].bitcast(I32), 0)
         make_identity(nc, ident[:])
 
         ms_view = mstore.rearrange("(p j) m -> p j m", j=PACK)
         vals_view = vals.rearrange("(p t) c -> t p c", t=PACK)
 
-        def load_key_scales(g):
+        nc.sync.dma_start(idx[:], offs)
+        nc.sync.dma_start(out=key_pool[:].bitcast(I32), in_=keys_words[0].bitcast(I32))
+        for g in range(4):
             nc.sync.dma_start(
                 out=key_pool_scales[32 * g : 32 * g + 4, :].bitcast(I32),
                 in_=keys_scales[0, 4 * g : 4 * g + 4, :].bitcast(I32),
             )
-
-        nc.sync.dma_start(out=wm_raw[:], in_=wm.rearrange("(p j) e -> p j e", j=PACK))
-        nc.sync.dma_start(out=ms_raw[0][:], in_=ms_view[:, :, 0:BANK])
-        nc.sync.dma_start(idx[:], offs)
-        nc.sync.dma_start(out=ms_raw[1][:], in_=ms_view[:, :, BANK : 2 * BANK])
-        load_key_scales(0)
-        load_key_scales(1)
         nc.sync.dma_start(out=q_raw[:], in_=query.rearrange("(p j) q -> p j q", j=PACK))
-        load_key_scales(2)
-        load_key_scales(3)
-        nc.sync.dma_start(out=key_pool[:].bitcast(I32), in_=keys_words[0].bitcast(I32))
         nc.sync.dma_start(idx2[:], offs2)
         nc.sync.dma_start(out=earl_rows[0][:], in_=earl[0:P, :])
         nc.sync.dma_start(out=factor[:], in_=slot_factor.rearrange("o (p t) -> p o t", t=PACK))
+        nc.sync.dma_start(out=wm_raw[:], in_=wm.rearrange("(p j) e -> p j e", j=PACK))
+        nc.sync.dma_start(out=ms_raw[0][:], in_=ms_view[:, :, 0:BANK])
+        nc.sync.dma_start(out=ms_raw[1][:], in_=ms_view[:, :, BANK : 2 * BANK])
         nc.sync.dma_start(out=earl_rows[1][:], in_=earl[P : 2 * P, :])
         nc.sync.dma_start(idx3[:], offs3)
         for t in range(PACK):
             nc.sync.dma_start(out=val_rows[t][:], in_=vals_view[t])
 
+        keys = sb.tile([P, I], U16, name="keys", align_bytes=64)
+        key_scales = sb.tile([P, I], U8, name="key_scales", align_bytes=64)
+        nc.vector.tensor_copy(out=keys[:], in_=key_pool[:].indirect(idx[:]))
+        nc.vector.tensor_copy(out=key_scales[:], in_=key_pool_scales[:].indirect(idx[:]))
+
+        q_bf = sb.tile([P, Q, PACK], BF16, name="q_bf", align_bytes=64)
+        interleave(nc.scalar.copy, q_bf[:], q_raw[:])
+        q_codes, q_scales = quantise("q", q_bf[:].rearrange("p c t -> p (c t)"), Q)
+        earl_g = [sb.tile([P, I], F32, name=f"earl_g{h}") for h in range(2)]
+        nc.scalar.activation(out=earl_g[0][:], in_=earl_rows[0][:].indirect(idx2[:]), func=COPY)
+
+        w_bf = sb.tile([P, Q, PACK], BF16, name="w_bf", align_bytes=64)
+        scores = []
+        for h in range(2):
+            rows = slice(h * P, (h + 1) * P)
+            scores.append(sc.tile([P, BANK], F32, name="score"))
+            nc.tensor.matmul_mx(
+                out=scores[h][:], lhsT=q_codes[:, rows].bitcast(FP8X4), lhsT_scale=q_scales[:, rows],
+                rhs=keys[:].bitcast(FP4X4), rhs_scale=key_scales[:], start=True, stop=True,
+            )
+
+        def weigh(h):
+            w = sb.tile([P, I], F32, name=f"w{h}")
+            nc.vector.tensor_tensor(out=w[:], in0=scores[h][:], in1=earl_g[h][:], op=MULT)
+            turned = tr.tile([P, PACK, P], F32, name="turned")
+            for t in range(PACK):
+                nc.tensor.transpose(turned[:, t, :], w[:, t:I:PACK], ident[:])
+            nc.vector.tensor_tensor(
+                out=w_bf[:, h * P : (h + 1) * P, :], in0=turned[:].rearrange("p t q -> p q t"),
+                in1=factor[:].to_broadcast([P, P, PACK]), op=MULT,
+            )
+
+        weigh(0)
+
         wm_bf = sb.tile([P, PACK * E], BF16, name="wm_bf", align_bytes=64)
-        nc.vector.tensor_copy(
-            out=wm_bf[:].rearrange("p (t m j) -> p m j t", t=PACK, j=PACK),
-            in_=wm_raw[:].rearrange("p j (m t) -> p m j t", t=PACK),
-        )
+        wm_dst = wm_bf[:].rearrange("p (t m j) -> p m j t", t=PACK, j=PACK)
+        wm_src = wm_raw[:].rearrange("p j (m t) -> p m j t", t=PACK)
+        nc.vector.tensor_copy(out=wm_dst[:, 0:88], in_=wm_src[:, 0:88])
+        nc.scalar.copy(out=wm_dst[:, 88:P], in_=wm_src[:, 88:P])
         wm_codes, wm_scales = quantise("wm", wm_bf[:], E)
         me = [sb.tile([P, M], F32, name=f"me{t}") for t in range(PACK)]
-        for h in range(2):
+
+        def quantise_store(h, split):
             ms_bf = sb.tile([P, BANK, PACK], BF16, name=f"ms_bf{h}", align_bytes=64)
-            interleave(nc.vector.tensor_copy, ms_bf[:], ms_raw[h][:])
-            ms_codes, ms_scales = quantise(f"ms{h}", ms_bf[:].rearrange("p c t -> p (c t)"), BANK)
+            interleave(nc.vector.tensor_copy, ms_bf[:, 0:split, :], ms_raw[h][:, :, 0:split])
+            if split < BANK:
+                interleave(nc.scalar.copy, ms_bf[:, split:BANK, :], ms_raw[h][:, :, split:BANK])
+            return quantise(f"ms{h}", ms_bf[:].rearrange("p c t -> p (c t)"), BANK)
+
+        def memories(h, ms_codes, ms_scales):
             for t in range(PACK):
                 cols = slice(t * P, (t + 1) * P)
                 acc = mm.tile([P, BANK], F32, name="acc")
@@ -107,70 +142,76 @@ def tile_attend_earliertable_remembered_lean_pl_kernel(
                 )
                 nc.scalar.copy(out=me[t][:, h * BANK : (h + 1) * BANK], in_=acc[:])
 
-        q_bf = sb.tile([P, Q, PACK], BF16, name="q_bf", align_bytes=64)
-        interleave(nc.vector.tensor_copy, q_bf[:], q_raw[:])
-        q_codes, q_scales = quantise("q", q_bf[:].rearrange("p c t -> p (c t)"), Q)
-        keys = sb.tile([P, I], U16, name="keys", align_bytes=64)
-        key_scales = sb.tile([P, I], U8, name="key_scales", align_bytes=64)
-        nc.vector.tensor_copy(out=keys[:], in_=key_pool[:].indirect(idx[:]))
-        nc.vector.tensor_copy(out=key_scales[:], in_=key_pool_scales[:].indirect(idx[:]))
-        w_bf = sb.tile([P, Q, PACK], BF16, name="w_bf", align_bytes=64)
-        for h in range(2):
-            rows = slice(h * P, (h + 1) * P)
-            earl_g = sb.tile([P, I], F32, name=f"earl_g{h}")
-            nc.scalar.activation(out=earl_g[:], in_=earl_rows[h][:].indirect(idx2[:]), func=COPY)
-            acc = mm.tile([P, BANK], F32, name="acc")
-            nc.tensor.matmul_mx(
-                out=acc[:], lhsT=q_codes[:, rows].bitcast(FP8X4), lhsT_scale=q_scales[:, rows],
-                rhs=keys[:].bitcast(FP4X4), rhs_scale=key_scales[:], start=True, stop=True,
-            )
-            w = sb.tile([P, I], F32, name=f"w{h}")
-            nc.vector.tensor_tensor(out=w[:], in0=acc[:], in1=earl_g[:], op=MULT)
-            turned = tr.tile([P, PACK, P], F32, name="turned")
-            for t in range(PACK):
-                nc.tensor.transpose(turned[:, t, :], w[:, t:I:PACK], ident[:])
-            nc.vector.tensor_tensor(
-                out=w_bf[:, rows, :], in0=turned[:].rearrange("p t q -> p q t"),
-                in1=factor[:].to_broadcast([P, P, PACK]), op=MULT,
-            )
+        ms0 = quantise_store(0, 304)
+        ms1 = quantise_store(1, 416)
+        memories(0, *ms0)
+        memories(1, *ms1)
+
+        nc.vector.tensor_copy(out=earl_g[1][:], in_=earl_rows[1][:].indirect(idx2[:]))
+        weigh(1)
         w_codes, w_scales = quantise("w", w_bf[:].rearrange("p c t -> p (c t)"), Q)
 
-        me_g = []
-        for t in range(PACK):
-            picked = sb.tile([P, Q], F32, name=f"me_g{t}")
-            nc.vector.tensor_copy(out=picked[:], in_=me[t][:].indirect(idx3[:]))
-            me_g.append(picked)
+        me_g = sb.tile([P, PACK, Q], F32, name="me_g")
+        for t in range(2):
+            nc.vector.tensor_copy(out=me_g[:, t, :], in_=me[t][:].indirect(idx3[:]))
 
+        val_g = [sb.tile([P, I], BF16, name=f"val_g{t}", tag=f"val_g{t}") for t in range(2)]
         y = sb.tile([P, PACK, Q], F32, name="y")
         out_rows = out_0.rearrange("(p t) q -> p t q", t=PACK)
-        for t in range(PACK):
-            val_g = sb.tile([P, I], BF16, name=f"val_g{t}")
-            if t < PACK - 1:
-                nc.scalar.activation(out=val_g[:], in_=val_rows[t][:].indirect(idx[:]), func=COPY)
-            else:
-                nc.vector.tensor_copy(out=val_g[:, 0 : I // 2], in_=val_rows[t][:].indirect(idx[:, 0:16]))
-                nc.scalar.activation(
-                    out=val_g[:, I // 2 : I], in_=val_rows[t][:].indirect(idx[:, 16:32]), func=COPY
-                )
-            words = val_g[:].bitcast(F32)
-            turned = tr.tile([P, 2, P], F32, name="turned")
+
+        def turn_values(t, turned):
+            words = val_g[t][:].bitcast(F32)
             for u in range(2):
                 nc.tensor.transpose(turned[:, u, :], words[:, u : I // 2 : 2], ident[:])
-            v_bf = sb.tile([P, P * PACK], BF16, name=f"v_bf{t}", align_bytes=64)
-            nc.vector.tensor_copy(
+
+        def value_product(out, codes, scales):
+            nc.tensor.matmul_mx(
+                out=out, lhsT=codes.bitcast(FP8X4), lhsT_scale=scales,
+                rhs=w_codes[:].bitcast(FP8X4), rhs_scale=w_scales[:], start=True, stop=True,
+            )
+
+        def scale_and_store(pair, sums):
+            rows = slice(2 * pair, 2 * pair + 2)
+            nc.vector.tensor_tensor(out=y[:, rows, :], in0=sums[:], in1=me_g[:, rows, :], op=MULT)
+            nc.sync.dma_start(out=out_rows[:, rows, :], in_=y[:, rows, :])
+
+        turned = mm.tile([P, 2, 2, P], F32, name="acc")
+        nc.vector.tensor_copy(out=val_g[0][:], in_=val_rows[0][:].indirect(idx[:]))
+        nc.scalar.activation(out=val_g[1][:], in_=val_rows[1][:].indirect(idx[:]), func=COPY)
+        for t in range(2):
+            turn_values(t, turned[:, t])
+        v_bf = sb.tile([P, 2 * P * PACK], BF16, name="v_bf01", tag="v_bf01", align_bytes=64)
+        nc.scalar.copy(
+            out=v_bf[:].bitcast(F32).rearrange("p (t e u) -> p t e u", t=2, u=2),
+            in_=turned[:].rearrange("p t u e -> p t e u"),
+        )
+        v_codes, v_scales = quantise("v01", v_bf[:], 2 * P)
+        sums = sc.tile([P, 2, Q], F32, name="score")
+        for t in range(2):
+            value_product(sums[:, t, :], v_codes[:, t * P : (t + 1) * P], v_scales[:, t * P : (t + 1) * P])
+        scale_and_store(0, sums)
+
+        val_g.append(sb.tile([P, I], BF16, name="val_g2", tag="val_g1"))
+        val_g.append(sb.tile([P, I], BF16, name="val_g3", tag="v_bf01", align_bytes=64))
+        nc.scalar.activation(out=val_g[2][:], in_=val_rows[2][:].indirect(idx[:]), func=COPY)
+        for t in range(2, PACK):
+            nc.scalar.activation(out=me_g[:, t, :], in_=me[t][:].indirect(idx3[:]), func=COPY)
+        nc.vector.tensor_copy(out=val_g[3][:, 0 : I // 2], in_=val_rows[3][:].indirect(idx[:, 0:16]))
+        nc.scalar.activation(
+            out=val_g[3][:, I // 2 : I], in_=val_rows[3][:].indirect(idx[:, 16:32]), func=COPY
+        )
+        sums = sc.tile([P, 2, Q], F32, name="score")
+        for t in range(2, PACK):
+            turned = tr.tile([P, 2, P], F32, name="turned")
+            turn_values(t, turned)
+            v_bf = sb.tile([P, P * PACK], BF16, name=f"v_bf{t}", tag=f"val_rows{5 - t}", align_bytes=64)
+            nc.scalar.copy(
                 out=v_bf[:].bitcast(F32).rearrange("p (e u) -> p e u", u=2),
                 in_=turned[:].rearrange("p u e -> p e u"),
             )
             v_codes, v_scales = quantise(f"v{t}", v_bf[:], P)
-            acc = mm.tile([P, Q], F32, name="acc")
-            nc.tensor.matmul_mx(
-                out=acc[:], lhsT=v_codes[:].bitcast(FP8X4), lhsT_scale=v_scales[:],
-                rhs=w_codes[:].bitcast(FP8X4), rhs_scale=w_scales[:], start=True, stop=True,
-            )
-            nc.vector.tensor_tensor(out=y[:, t, :], in0=acc[:], in1=me_g[t][:], op=MULT)
-            if t == PACK - 2:
-                nc.sync.dma_start(out=out_rows[:, 0 : PACK - 1, :], in_=y[:, 0 : PACK - 1, :])
-        nc.sync.dma_start(out=out_rows[:, PACK - 1, :], in_=y[:, PACK - 1, :])
+            value_product(sums[:, t - 2, :], v_codes[:], v_scales[:])
+        scale_and_store(1, sums)
 
         y_bf = sb.tile([P, Q, PACK], BF16, name="y_bf", align_bytes=64)
         split = 160

@@ -29,6 +29,7 @@ def tile_attend_earliertable_remembered_lean_pl_kernel(
     nc = tc.nc
     with ExitStack() as ctx:
         sb = ctx.enter_context(tc.tile_pool(name="sb", bufs=1))
+        late = ctx.enter_context(tc.tile_pool(name="late", bufs=1))
         mm = ctx.enter_context(tc.psum_pool(name="mm", bufs=4))
         sc = ctx.enter_context(tc.psum_pool(name="sc", bufs=2))
         tr = ctx.enter_context(tc.psum_pool(name="tr", bufs=2))
@@ -54,7 +55,10 @@ def tile_attend_earliertable_remembered_lean_pl_kernel(
         key_pool = sb.tile([P, T], U16, name="key_pool")
         key_pool_scales = sb.tile([P, T], U8, name="key_pool_scales")
         earl_rows = [sb.tile([P, Z], F32, name=f"earl_rows{h}") for h in range(2)]
-        val_rows = [sb.tile([P, T], F32, name=f"val_rows{t}", tag=f"val_rows{t}", align_bytes=64) for t in range(PACK)]
+        val_rows = [late.tile([P, T], F32, name="val_rows0", offset=8192, align_bytes=64)]
+        for t in range(1, PACK - 1):
+            val_rows.append(sb.tile([P, T], F32, name=f"val_rows{t}", tag=f"val_rows{t}", align_bytes=64))
+        val_rows.append(late.tile([P, T], F32, name="val_rows3", offset=0, align_bytes=64))
         factor = sb.tile([P, 1, PACK], F32, name="factor")
         ident = sb.tile([P, P], F32, name="ident")
 
@@ -66,16 +70,16 @@ def tile_attend_earliertable_remembered_lean_pl_kernel(
 
         nc.sync.dma_start(idx[:], offs)
         nc.sync.dma_start(out=key_pool[:].bitcast(I32), in_=keys_words[0].bitcast(I32))
+        nc.sync.dma_start(out=q_raw[:], in_=query.rearrange("(p j) q -> p j q", j=PACK))
         for g in range(4):
             nc.sync.dma_start(
                 out=key_pool_scales[32 * g : 32 * g + 4, :].bitcast(I32),
                 in_=keys_scales[0, 4 * g : 4 * g + 4, :].bitcast(I32),
             )
-        nc.sync.dma_start(out=q_raw[:], in_=query.rearrange("(p j) q -> p j q", j=PACK))
-        nc.sync.dma_start(idx2[:], offs2)
         nc.sync.dma_start(out=earl_rows[0][:], in_=earl[0:P, :])
-        nc.sync.dma_start(out=factor[:], in_=slot_factor.rearrange("o (p t) -> p o t", t=PACK))
+        nc.sync.dma_start(idx2[:], offs2)
         nc.sync.dma_start(out=wm_raw[:], in_=wm.rearrange("(p j) e -> p j e", j=PACK))
+        nc.sync.dma_start(out=factor[:], in_=slot_factor.rearrange("o (p t) -> p o t", t=PACK))
         nc.sync.dma_start(out=ms_raw[0][:], in_=ms_view[:, :, 0:BANK])
         nc.sync.dma_start(out=ms_raw[1][:], in_=ms_view[:, :, BANK : 2 * BANK])
         nc.sync.dma_start(out=earl_rows[1][:], in_=earl[P : 2 * P, :])
@@ -94,7 +98,8 @@ def tile_attend_earliertable_remembered_lean_pl_kernel(
         earl_g = [sb.tile([P, I], F32, name=f"earl_g{h}") for h in range(2)]
         nc.scalar.activation(out=earl_g[0][:], in_=earl_rows[0][:].indirect(idx2[:]), func=COPY)
 
-        w_bf = sb.tile([P, Q, PACK], BF16, name="w_bf", align_bytes=64)
+        w_codes = sb.tile([P, Q], U32, name="w_codes", align_bytes=64)
+        w_scales = sb.tile([P, Q], U8, name="w_scales", align_bytes=64)
         scores = []
         for h in range(2):
             rows = slice(h * P, (h + 1) * P)
@@ -107,15 +112,23 @@ def tile_attend_earliertable_remembered_lean_pl_kernel(
         def weigh(h):
             w = sb.tile([P, I], F32, name=f"w{h}")
             nc.vector.tensor_tensor(out=w[:], in0=scores[h][:], in1=earl_g[h][:], op=MULT)
+            return w
+
+        def turn_weights(h, w, w_bf):
             turned = tr.tile([P, PACK, P], F32, name="turned")
             for t in range(PACK):
                 nc.tensor.transpose(turned[:, t, :], w[:, t:I:PACK], ident[:])
             nc.vector.tensor_tensor(
-                out=w_bf[:, h * P : (h + 1) * P, :], in0=turned[:].rearrange("p t q -> p q t"),
+                out=w_bf[:], in0=turned[:].rearrange("p t q -> p q t"),
                 in1=factor[:].to_broadcast([P, P, PACK]), op=MULT,
             )
+            rows = slice(h * P, (h + 1) * P)
+            nc.vector.quantize_mx(
+                out=w_codes[:, rows].bitcast(FP8X4), scales=w_scales[:, rows],
+                in_=w_bf[:].rearrange("p c t -> p (c t)"),
+            )
 
-        weigh(0)
+        turn_weights(0, weigh(0), sb.tile([P, P, PACK], BF16, name="w_bf0", align_bytes=64))
 
         wm_bf = sb.tile([P, PACK * E], BF16, name="wm_bf", align_bytes=64)
         wm_dst = wm_bf[:].rearrange("p (t m j) -> p m j t", t=PACK, j=PACK)
@@ -148,15 +161,16 @@ def tile_attend_earliertable_remembered_lean_pl_kernel(
         memories(1, *ms1)
 
         nc.vector.tensor_copy(out=earl_g[1][:], in_=earl_rows[1][:].indirect(idx2[:]))
-        weigh(1)
-        w_codes, w_scales = quantise("w", w_bf[:].rearrange("p c t -> p (c t)"), Q)
+        w1 = weigh(1)
+        val_g = [sb.tile([P, I], BF16, name=f"val_g{t}", tag=f"val_g{t}") for t in range(2)]
+        nc.vector.tensor_copy(out=val_g[0][:], in_=val_rows[0][:].indirect(idx[:]))
+        turn_weights(1, w1, late.tile([P, P, PACK], BF16, name="w_bf1", offset=8192, align_bytes=64))
 
-        me_g = sb.tile([P, PACK, Q], F32, name="me_g")
-        for t in range(2):
+        me_g = late.tile([P, PACK - 1, Q], F32, name="me_g", offset=8192 + 1024, align_bytes=64)
+        for t in range(PACK - 1):
             nc.vector.tensor_copy(out=me_g[:, t, :], in_=me[t][:].indirect(idx3[:]))
 
-        val_g = [sb.tile([P, I], BF16, name=f"val_g{t}", tag=f"val_g{t}") for t in range(2)]
-        y = sb.tile([P, PACK, Q], F32, name="y")
+        y = late.tile([P, PACK, Q], F32, name="y", offset=0, align_bytes=64)
         out_rows = out_0.rearrange("(p t) q -> p t q", t=PACK)
 
         def turn_values(t, turned):
@@ -170,17 +184,17 @@ def tile_attend_earliertable_remembered_lean_pl_kernel(
                 rhs=w_codes[:].bitcast(FP8X4), rhs_scale=w_scales[:], start=True, stop=True,
             )
 
-        def scale_and_store(pair, sums):
-            rows = slice(2 * pair, 2 * pair + 2)
-            nc.vector.tensor_tensor(out=y[:, rows, :], in0=sums[:], in1=me_g[:, rows, :], op=MULT)
+        def scale_and_store(rows, sums, memory):
+            nc.vector.tensor_tensor(out=y[:, rows, :], in0=sums[:], in1=memory, op=MULT)
             nc.sync.dma_start(out=out_rows[:, rows, :], in_=y[:, rows, :])
 
         turned = mm.tile([P, 2, 2, P], F32, name="acc")
-        nc.vector.tensor_copy(out=val_g[0][:], in_=val_rows[0][:].indirect(idx[:]))
         nc.scalar.activation(out=val_g[1][:], in_=val_rows[1][:].indirect(idx[:]), func=COPY)
+        me_g_last = sb.tile([P, 1, Q], F32, name="me_g_last", tag="val_rows1", align_bytes=64)
+        nc.scalar.activation(out=me_g_last[:, 0, :], in_=me[PACK - 1][:].indirect(idx3[:]), func=COPY)
         for t in range(2):
             turn_values(t, turned[:, t])
-        v_bf = sb.tile([P, 2 * P * PACK], BF16, name="v_bf01", tag="v_bf01", align_bytes=64)
+        v_bf = sb.tile([P, 2 * P * PACK], BF16, name="v_bf01", align_bytes=64)
         nc.scalar.copy(
             out=v_bf[:].bitcast(F32).rearrange("p (t e u) -> p t e u", t=2, u=2),
             in_=turned[:].rearrange("p t u e -> p t e u"),
@@ -189,29 +203,31 @@ def tile_attend_earliertable_remembered_lean_pl_kernel(
         sums = sc.tile([P, 2, Q], F32, name="score")
         for t in range(2):
             value_product(sums[:, t, :], v_codes[:, t * P : (t + 1) * P], v_scales[:, t * P : (t + 1) * P])
-        scale_and_store(0, sums)
+        first_sums = sums
 
         val_g.append(sb.tile([P, I], BF16, name="val_g2", tag="val_g1"))
-        val_g.append(sb.tile([P, I], BF16, name="val_g3", tag="v_bf01", align_bytes=64))
+        val_g.append(sb.tile([P, I], BF16, name="val_g3"))
         nc.scalar.activation(out=val_g[2][:], in_=val_rows[2][:].indirect(idx[:]), func=COPY)
-        for t in range(2, PACK):
-            nc.scalar.activation(out=me_g[:, t, :], in_=me[t][:].indirect(idx3[:]), func=COPY)
         nc.vector.tensor_copy(out=val_g[3][:, 0 : I // 2], in_=val_rows[3][:].indirect(idx[:, 0:16]))
         nc.scalar.activation(
             out=val_g[3][:, I // 2 : I], in_=val_rows[3][:].indirect(idx[:, 16:32]), func=COPY
         )
-        sums = sc.tile([P, 2, Q], F32, name="score")
+        scale_and_store(slice(0, 2), first_sums, me_g[:, 0:2, :])
+        late_sums = []
         for t in range(2, PACK):
             turned = tr.tile([P, 2, P], F32, name="turned")
             turn_values(t, turned)
-            v_bf = sb.tile([P, P * PACK], BF16, name=f"v_bf{t}", tag=f"val_rows{5 - t}", align_bytes=64)
+            v_bf = late.tile([P, P * PACK], BF16, name=f"v_bf{t}", offset=4096 + 1024 * (t - 2), align_bytes=64)
             nc.scalar.copy(
                 out=v_bf[:].bitcast(F32).rearrange("p (e u) -> p e u", u=2),
                 in_=turned[:].rearrange("p u e -> p e u"),
             )
             v_codes, v_scales = quantise(f"v{t}", v_bf[:], P)
-            value_product(sums[:, t - 2, :], v_codes[:], v_scales[:])
-        scale_and_store(1, sums)
+            sums = mm.tile([P, 1, Q], F32, name="acc")
+            value_product(sums[:, 0, :], v_codes[:], v_scales[:])
+            late_sums.append(sums)
+        scale_and_store(slice(2, 3), late_sums[0], me_g[:, 2:3, :])
+        scale_and_store(slice(3, 4), late_sums[1], me_g_last[:])
 
         y_bf = sb.tile([P, Q, PACK], BF16, name="y_bf", align_bytes=64)
         split = 160

@@ -20,6 +20,21 @@ COPY = mybir.ActivationFunctionType.Copy
 P = 128
 PACK = 4
 BANK = 512
+QUADRANT = 32
+SCALE_ROWS = 16
+STRIPE = 16
+RUN = 4
+LAST = PACK - 1
+
+WM_ON_VECTOR = 88
+STORE_ON_VECTOR = (304, 416)
+Y_ON_VECTOR = 160
+
+VAL_BYTES = 4 * T
+ON_LAST_VALUES = 0
+ON_FIRST_VALUES = VAL_BYTES
+Y_BYTES = 4 * PACK * Q
+GROUPED_BYTES = 2 * P * PACK
 
 
 def tile_attend_earliertable_remembered_lean_pl_kernel(
@@ -42,23 +57,23 @@ def tile_attend_earliertable_remembered_lean_pl_kernel(
 
         def interleave(engine_copy, dst, src):
             engine_copy(
-                out=dst.rearrange("p (c i) t -> p c t i", i=4),
-                in_=src.rearrange("p t (c i) -> p c t i", i=4),
+                out=dst.rearrange("p (c i) t -> p c t i", i=RUN),
+                in_=src.rearrange("p t (c i) -> p c t i", i=RUN),
             )
 
-        idx = sb.tile([P, I // 16], U16, name="idx")
-        idx2 = sb.tile([P, I // 16], U16, name="idx2")
-        idx3 = sb.tile([P, Q // 16], U16, name="idx3")
+        idx = sb.tile([P, I // STRIPE], U16, name="idx")
+        idx2 = sb.tile([P, I // STRIPE], U16, name="idx2")
+        idx3 = sb.tile([P, Q // STRIPE], U16, name="idx3")
         wm_raw = sb.tile([P, PACK, E], F32, name="wm_raw")
         ms_raw = [sb.tile([P, PACK, BANK], F32, name=f"ms_raw{h}") for h in range(2)]
         q_raw = sb.tile([P, PACK, Q], F32, name="q_raw")
         key_pool = sb.tile([P, T], U16, name="key_pool")
         key_pool_scales = sb.tile([P, T], U8, name="key_pool_scales")
         earl_rows = [sb.tile([P, Z], F32, name=f"earl_rows{h}") for h in range(2)]
-        val_rows = [late.tile([P, T], F32, name="val_rows0", offset=8192, align_bytes=64)]
-        for t in range(1, PACK - 1):
+        val_rows = [late.tile([P, T], F32, name="val_rows0", offset=ON_FIRST_VALUES, align_bytes=64)]
+        for t in range(1, LAST):
             val_rows.append(sb.tile([P, T], F32, name=f"val_rows{t}", tag=f"val_rows{t}", align_bytes=64))
-        val_rows.append(late.tile([P, T], F32, name="val_rows3", offset=0, align_bytes=64))
+        val_rows.append(late.tile([P, T], F32, name="val_rows3", offset=ON_LAST_VALUES, align_bytes=64))
         factor = sb.tile([P, 1, PACK], F32, name="factor")
         ident = sb.tile([P, P], F32, name="ident")
 
@@ -68,21 +83,21 @@ def tile_attend_earliertable_remembered_lean_pl_kernel(
         ms_view = mstore.rearrange("(p j) m -> p j m", j=PACK)
         vals_view = vals.rearrange("(p t) c -> t p c", t=PACK)
 
-        nc.sync.dma_start(idx[:], offs)
         nc.sync.dma_start(out=key_pool[:].bitcast(I32), in_=keys_words[0].bitcast(I32))
+        nc.sync.dma_start(idx[:], offs)
         nc.sync.dma_start(out=q_raw[:], in_=query.rearrange("(p j) q -> p j q", j=PACK))
-        for g in range(4):
+        for r in range(PACK):
             nc.sync.dma_start(
-                out=key_pool_scales[32 * g : 32 * g + 4, :].bitcast(I32),
-                in_=keys_scales[0, 4 * g : 4 * g + 4, :].bitcast(I32),
+                out=key_pool_scales[r:P:QUADRANT, :].bitcast(I32),
+                in_=keys_scales[0, r:SCALE_ROWS:PACK, :].bitcast(I32),
             )
         nc.sync.dma_start(out=earl_rows[0][:], in_=earl[0:P, :])
         nc.sync.dma_start(idx2[:], offs2)
         nc.sync.dma_start(out=wm_raw[:], in_=wm.rearrange("(p j) e -> p j e", j=PACK))
         nc.sync.dma_start(out=factor[:], in_=slot_factor.rearrange("o (p t) -> p o t", t=PACK))
         nc.sync.dma_start(out=ms_raw[0][:], in_=ms_view[:, :, 0:BANK])
-        nc.sync.dma_start(out=ms_raw[1][:], in_=ms_view[:, :, BANK : 2 * BANK])
-        nc.sync.dma_start(out=earl_rows[1][:], in_=earl[P : 2 * P, :])
+        nc.sync.dma_start(out=ms_raw[1][:], in_=ms_view[:, :, BANK:M])
+        nc.sync.dma_start(out=earl_rows[1][:], in_=earl[P:Q, :])
         nc.sync.dma_start(idx3[:], offs3)
         for t in range(PACK):
             nc.sync.dma_start(out=val_rows[t][:], in_=vals_view[t])
@@ -102,10 +117,10 @@ def tile_attend_earliertable_remembered_lean_pl_kernel(
         w_scales = sb.tile([P, Q], U8, name="w_scales", align_bytes=64)
         scores = []
         for h in range(2):
-            rows = slice(h * P, (h + 1) * P)
+            q_rows = slice(h * P, (h + 1) * P)
             scores.append(sc.tile([P, BANK], F32, name="score"))
             nc.tensor.matmul_mx(
-                out=scores[h][:], lhsT=q_codes[:, rows].bitcast(FP8X4), lhsT_scale=q_scales[:, rows],
+                out=scores[h][:], lhsT=q_codes[:, q_rows].bitcast(FP8X4), lhsT_scale=q_scales[:, q_rows],
                 rhs=keys[:].bitcast(FP4X4), rhs_scale=key_scales[:], start=True, stop=True,
             )
 
@@ -122,61 +137,62 @@ def tile_attend_earliertable_remembered_lean_pl_kernel(
                 out=w_bf[:], in0=turned[:].rearrange("p t q -> p q t"),
                 in1=factor[:].to_broadcast([P, P, PACK]), op=MULT,
             )
-            rows = slice(h * P, (h + 1) * P)
+            q_rows = slice(h * P, (h + 1) * P)
             nc.vector.quantize_mx(
-                out=w_codes[:, rows].bitcast(FP8X4), scales=w_scales[:, rows],
+                out=w_codes[:, q_rows].bitcast(FP8X4), scales=w_scales[:, q_rows],
                 in_=w_bf[:].rearrange("p c t -> p (c t)"),
             )
 
         turn_weights(0, weigh(0), sb.tile([P, P, PACK], BF16, name="w_bf0", align_bytes=64))
 
         wm_bf = sb.tile([P, PACK * E], BF16, name="wm_bf", align_bytes=64)
-        wm_dst = wm_bf[:].rearrange("p (t m j) -> p m j t", t=PACK, j=PACK)
-        wm_src = wm_raw[:].rearrange("p j (m t) -> p m j t", t=PACK)
-        nc.vector.tensor_copy(out=wm_dst[:, 0:88], in_=wm_src[:, 0:88])
-        nc.scalar.copy(out=wm_dst[:, 88:P], in_=wm_src[:, 88:P])
+        wm_dst = wm_bf[:].rearrange("p (t m j) -> p m t j", t=PACK, j=PACK)
+        wm_src = wm_raw[:].rearrange("p j (m t) -> p m t j", t=PACK)
+        nc.vector.tensor_copy(out=wm_dst[:, 0:WM_ON_VECTOR], in_=wm_src[:, 0:WM_ON_VECTOR])
+        nc.scalar.copy(out=wm_dst[:, WM_ON_VECTOR:P], in_=wm_src[:, WM_ON_VECTOR:P])
         wm_codes, wm_scales = quantise("wm", wm_bf[:], E)
         me = [sb.tile([P, M], F32, name=f"me{t}") for t in range(PACK)]
 
-        def quantise_store(h, split):
+        def quantise_store(h):
+            share = STORE_ON_VECTOR[h]
             ms_bf = sb.tile([P, BANK, PACK], BF16, name=f"ms_bf{h}", align_bytes=64)
-            interleave(nc.vector.tensor_copy, ms_bf[:, 0:split, :], ms_raw[h][:, :, 0:split])
-            if split < BANK:
-                interleave(nc.scalar.copy, ms_bf[:, split:BANK, :], ms_raw[h][:, :, split:BANK])
+            interleave(nc.vector.tensor_copy, ms_bf[:, 0:share, :], ms_raw[h][:, :, 0:share])
+            interleave(nc.scalar.copy, ms_bf[:, share:BANK, :], ms_raw[h][:, :, share:BANK])
             return quantise(f"ms{h}", ms_bf[:].rearrange("p c t -> p (c t)"), BANK)
 
         def memories(h, ms_codes, ms_scales):
             for t in range(PACK):
-                cols = slice(t * P, (t + 1) * P)
+                features = slice(t * P, (t + 1) * P)
                 acc = mm.tile([P, BANK], F32, name="acc")
                 nc.tensor.matmul_mx(
-                    out=acc[:], lhsT=wm_codes[:, cols].bitcast(FP8X4), lhsT_scale=wm_scales[:, cols],
+                    out=acc[:], lhsT=wm_codes[:, features].bitcast(FP8X4), lhsT_scale=wm_scales[:, features],
                     rhs=ms_codes[:].bitcast(FP8X4), rhs_scale=ms_scales[:], start=True, stop=True,
                 )
                 nc.scalar.copy(out=me[t][:, h * BANK : (h + 1) * BANK], in_=acc[:])
 
-        ms0 = quantise_store(0, 304)
-        ms1 = quantise_store(1, 416)
-        memories(0, *ms0)
-        memories(1, *ms1)
+        store_halves = [quantise_store(h) for h in range(2)]
+        for h in range(2):
+            memories(h, *store_halves[h])
 
         nc.vector.tensor_copy(out=earl_g[1][:], in_=earl_rows[1][:].indirect(idx2[:]))
         w1 = weigh(1)
         val_g = [sb.tile([P, I], BF16, name=f"val_g{t}", tag=f"val_g{t}") for t in range(2)]
         nc.vector.tensor_copy(out=val_g[0][:], in_=val_rows[0][:].indirect(idx[:]))
-        turn_weights(1, w1, late.tile([P, P, PACK], BF16, name="w_bf1", offset=8192, align_bytes=64))
+        turn_weights(1, w1, late.tile([P, P, PACK], BF16, name="w_bf1", offset=ON_FIRST_VALUES, align_bytes=64))
 
-        me_g = late.tile([P, PACK - 1, Q], F32, name="me_g", offset=8192 + 1024, align_bytes=64)
-        for t in range(PACK - 1):
+        me_g = late.tile(
+            [P, LAST, Q], F32, name="me_g", offset=ON_FIRST_VALUES + GROUPED_BYTES, align_bytes=64
+        )
+        for t in range(LAST):
             nc.vector.tensor_copy(out=me_g[:, t, :], in_=me[t][:].indirect(idx3[:]))
 
-        y = late.tile([P, PACK, Q], F32, name="y", offset=0, align_bytes=64)
+        y = late.tile([P, PACK, Q], F32, name="y", offset=ON_LAST_VALUES, align_bytes=64)
         out_rows = out_0.rearrange("(p t) q -> p t q", t=PACK)
 
         def turn_values(t, turned):
-            words = val_g[t][:].bitcast(F32)
+            pairs = val_g[t][:].bitcast(F32)
             for u in range(2):
-                nc.tensor.transpose(turned[:, u, :], words[:, u : I // 2 : 2], ident[:])
+                nc.tensor.transpose(turned[:, u, :], pairs[:, u : I // 2 : 2], ident[:])
 
         def value_product(out, codes, scales):
             nc.tensor.matmul_mx(
@@ -184,40 +200,48 @@ def tile_attend_earliertable_remembered_lean_pl_kernel(
                 rhs=w_codes[:].bitcast(FP8X4), rhs_scale=w_scales[:], start=True, stop=True,
             )
 
-        def scale_and_store(rows, sums, memory):
-            nc.vector.tensor_tensor(out=y[:, rows, :], in0=sums[:], in1=memory, op=MULT)
-            nc.sync.dma_start(out=out_rows[:, rows, :], in_=y[:, rows, :])
+        def scale_and_store(tiles, sums, memory):
+            nc.vector.tensor_tensor(out=y[:, tiles, :], in0=sums[:], in1=memory, op=MULT)
+            nc.sync.dma_start(out=out_rows[:, tiles, :], in_=y[:, tiles, :])
 
-        turned = mm.tile([P, 2, 2, P], F32, name="acc")
+        turned_pair = mm.tile([P, 2, 2, P], F32, name="acc")
         nc.scalar.activation(out=val_g[1][:], in_=val_rows[1][:].indirect(idx[:]), func=COPY)
         me_g_last = sb.tile([P, 1, Q], F32, name="me_g_last", tag="val_rows1", align_bytes=64)
-        nc.scalar.activation(out=me_g_last[:, 0, :], in_=me[PACK - 1][:].indirect(idx3[:]), func=COPY)
+        nc.scalar.activation(out=me_g_last[:, 0, :], in_=me[LAST][:].indirect(idx3[:]), func=COPY)
         for t in range(2):
-            turn_values(t, turned[:, t])
-        v_bf = sb.tile([P, 2 * P * PACK], BF16, name="v_bf01", align_bytes=64)
+            turn_values(t, turned_pair[:, t])
+        pair_bf = sb.tile([P, 2 * P * PACK], BF16, name="v_bf01", align_bytes=64)
         nc.scalar.copy(
-            out=v_bf[:].bitcast(F32).rearrange("p (t e u) -> p t e u", t=2, u=2),
-            in_=turned[:].rearrange("p t u e -> p t e u"),
+            out=pair_bf[:].bitcast(F32).rearrange("p (t e u) -> p t e u", t=2, u=2),
+            in_=turned_pair[:].rearrange("p t u e -> p t e u"),
         )
-        v_codes, v_scales = quantise("v01", v_bf[:], 2 * P)
-        sums = sc.tile([P, 2, Q], F32, name="score")
+        pair_codes, pair_scales = quantise("v01", pair_bf[:], 2 * P)
+        pair_sums = sc.tile([P, 2, Q], F32, name="score")
         for t in range(2):
-            value_product(sums[:, t, :], v_codes[:, t * P : (t + 1) * P], v_scales[:, t * P : (t + 1) * P])
-        first_sums = sums
+            features = slice(t * P, (t + 1) * P)
+            value_product(pair_sums[:, t, :], pair_codes[:, features], pair_scales[:, features])
 
         val_g.append(sb.tile([P, I], BF16, name="val_g2", tag="val_g1"))
         val_g.append(sb.tile([P, I], BF16, name="val_g3"))
+        half, half_columns = I // 2, I // 2 // STRIPE
         nc.scalar.activation(out=val_g[2][:], in_=val_rows[2][:].indirect(idx[:]), func=COPY)
-        nc.vector.tensor_copy(out=val_g[3][:, 0 : I // 2], in_=val_rows[3][:].indirect(idx[:, 0:16]))
-        nc.scalar.activation(
-            out=val_g[3][:, I // 2 : I], in_=val_rows[3][:].indirect(idx[:, 16:32]), func=COPY
+        nc.vector.tensor_copy(
+            out=val_g[LAST][:, 0:half], in_=val_rows[LAST][:].indirect(idx[:, 0:half_columns])
         )
-        scale_and_store(slice(0, 2), first_sums, me_g[:, 0:2, :])
-        late_sums = []
+        nc.scalar.activation(
+            out=val_g[LAST][:, half:I], in_=val_rows[LAST][:].indirect(idx[:, half_columns : I // STRIPE]),
+            func=COPY,
+        )
+        scale_and_store(slice(0, 2), pair_sums, me_g[:, 0:2, :])
+
+        single_sums = []
         for t in range(2, PACK):
             turned = tr.tile([P, 2, P], F32, name="turned")
             turn_values(t, turned)
-            v_bf = late.tile([P, P * PACK], BF16, name=f"v_bf{t}", offset=4096 + 1024 * (t - 2), align_bytes=64)
+            v_bf = late.tile(
+                [P, P * PACK], BF16, name=f"v_bf{t}",
+                offset=ON_LAST_VALUES + Y_BYTES + GROUPED_BYTES * (t - 2), align_bytes=64,
+            )
             nc.scalar.copy(
                 out=v_bf[:].bitcast(F32).rearrange("p (e u) -> p e u", u=2),
                 in_=turned[:].rearrange("p u e -> p e u"),
@@ -225,21 +249,20 @@ def tile_attend_earliertable_remembered_lean_pl_kernel(
             v_codes, v_scales = quantise(f"v{t}", v_bf[:], P)
             sums = mm.tile([P, 1, Q], F32, name="acc")
             value_product(sums[:, 0, :], v_codes[:], v_scales[:])
-            late_sums.append(sums)
-        scale_and_store(slice(2, 3), late_sums[0], me_g[:, 2:3, :])
-        scale_and_store(slice(3, 4), late_sums[1], me_g_last[:])
+            single_sums.append(sums)
+        scale_and_store(slice(2, LAST), single_sums[0], me_g[:, 2:LAST, :])
+        scale_and_store(slice(LAST, PACK), single_sums[1], me_g_last[:])
 
         y_bf = sb.tile([P, Q, PACK], BF16, name="y_bf", align_bytes=64)
-        split = 160
-        interleave(nc.vector.tensor_copy, y_bf[:, 0:split, :], y[:, :, 0:split])
-        interleave(nc.scalar.copy, y_bf[:, split:Q, :], y[:, :, split:Q])
+        interleave(nc.vector.tensor_copy, y_bf[:, 0:Y_ON_VECTOR, :], y[:, :, 0:Y_ON_VECTOR])
+        interleave(nc.scalar.copy, y_bf[:, Y_ON_VECTOR:Q, :], y[:, :, Y_ON_VECTOR:Q])
         y_codes, y_scales = quantise("y", y_bf[:].rearrange("p c t -> p (c t)"), Q)
         nc.sync.dma_start(
             out=out_1[0].rearrange("p c r -> p (c r)").bitcast(I32), in_=y_codes[:].bitcast(I32)
         )
-        for g in range(4):
+        for g in range(P // QUADRANT):
             queue = nc.scalar if g % 2 == 0 else nc.sync
             queue.dma_start(
-                out=out_2[0, 4 * g : 4 * g + 4, :].bitcast(I32),
-                in_=y_scales[32 * g : 32 * g + 4, :].bitcast(I32),
+                out=out_2[0, PACK * g : PACK * (g + 1), :].bitcast(I32),
+                in_=y_scales[QUADRANT * g : QUADRANT * g + PACK, :].bitcast(I32),
             )

from contextlib import ExitStack

import concourse.mybir as mybir
from concourse.masks import make_identity

D, T, I, Q, E, Z, M, C = 512, 2048, 512, 256, 512, 1024, 1024, 512
FLOPS = 2 * (D * Q * I + I * E * Q + C * E * M)

F32 = mybir.dt.float32
BF16 = mybir.dt.bfloat16
I32 = mybir.dt.int32
U32 = mybir.dt.uint32
U16 = mybir.dt.uint16
U8 = mybir.dt.uint8
FP8X4 = mybir.dt.float8_e4m3fn_x4
FP4X4 = mybir.dt.float4_e2m1fn_x4
MULT = mybir.AluOpType.mult
COPY = mybir.ActivationFunctionType.Copy

P = 128
PACK = 4
BANK = 512
QUADRANT = 32
SCALE_ROWS = 16
STRIPE = 16
RUN = 4
LAST = PACK - 1

WM_ON_VECTOR = 88
STORE_ON_VECTOR = (304, 416)
Y_ON_VECTOR = 160

VAL_BYTES = 4 * T
ON_LAST_VALUES = 0
ON_FIRST_VALUES = VAL_BYTES
Y_BYTES = 4 * PACK * Q
GROUPED_BYTES = 2 * P * PACK


def tile_attend_earliertable_remembered_lean_pl_kernel(
    tc, query, keys_words, keys_scales, earl, slot_factor, vals, wm, mstore, offs, offs2, offs3,
    out_0, out_1, out_2,
):
    nc = tc.nc
    with ExitStack() as ctx:
        sb = ctx.enter_context(tc.tile_pool(name="sb", bufs=1))
        late = ctx.enter_context(tc.tile_pool(name="late", bufs=1))
        mm = ctx.enter_context(tc.psum_pool(name="mm", bufs=4))
        sc = ctx.enter_context(tc.psum_pool(name="sc", bufs=2))
        tr = ctx.enter_context(tc.psum_pool(name="tr", bufs=2))

        def quantise(name, grouped, width):
            codes = sb.tile([P, width], U32, name=name + "_codes", align_bytes=64)
            scales = sb.tile([P, width], U8, name=name + "_scales", align_bytes=64)
            nc.vector.quantize_mx(out=codes[:].bitcast(FP8X4), scales=scales[:], in_=grouped)
            return codes, scales

        def interleave(engine_copy, dst, src):
            engine_copy(
                out=dst.rearrange("p (c i) t -> p c t i", i=RUN),
                in_=src.rearrange("p t (c i) -> p c t i", i=RUN),
            )

        idx = sb.tile([P, I // STRIPE], U16, name="idx")
        idx2 = sb.tile([P, I // STRIPE], U16, name="idx2")
        idx3 = sb.tile([P, Q // STRIPE], U16, name="idx3")
        wm_raw = sb.tile([P, PACK, E], F32, name="wm_raw")
        ms_raw = [sb.tile([P, PACK, BANK], F32, name=f"ms_raw{h}") for h in range(2)]
        q_raw = sb.tile([P, PACK, Q], F32, name="q_raw")
        key_pool = sb.tile([P, T], U16, name="key_pool")
        key_pool_scales = sb.tile([P, T], U8, name="key_pool_scales")
        earl_rows = [sb.tile([P, Z], F32, name=f"earl_rows{h}") for h in range(2)]
        val_rows = [late.tile([P, T], F32, name="val_rows0", offset=ON_FIRST_VALUES, align_bytes=64)]
        for t in range(1, LAST):
            val_rows.append(sb.tile([P, T], F32, name=f"val_rows{t}", tag=f"val_rows{t}", align_bytes=64))
        val_rows.append(late.tile([P, T], F32, name="val_rows3", offset=ON_LAST_VALUES, align_bytes=64))
        factor = sb.tile([P, 1, PACK], F32, name="factor")
        ident = sb.tile([P, P], F32, name="ident")

        nc.gpsimd.memset(key_pool_scales[:].bitcast(I32), 0)
        make_identity(nc, ident[:])

        ms_view = mstore.rearrange("(p j) m -> p j m", j=PACK)
        vals_view = vals.rearrange("(p t) c -> t p c", t=PACK)

        nc.sync.dma_start(out=key_pool[:].bitcast(I32), in_=keys_words[0].bitcast(I32))
        nc.sync.dma_start(idx[:], offs)
        nc.sync.dma_start(out=q_raw[:], in_=query.rearrange("(p j) q -> p j q", j=PACK))
        for r in range(PACK):
            nc.sync.dma_start(
                out=key_pool_scales[r:P:QUADRANT, :].bitcast(I32),
                in_=keys_scales[0, r:SCALE_ROWS:PACK, :].bitcast(I32),
            )
        nc.sync.dma_start(out=earl_rows[0][:], in_=earl[0:P, :])
        nc.sync.dma_start(idx2[:], offs2)
        nc.sync.dma_start(out=wm_raw[:], in_=wm.rearrange("(p j) e -> p j e", j=PACK))
        nc.sync.dma_start(out=factor[:], in_=slot_factor.rearrange("o (p t) -> p o t", t=PACK))
        nc.sync.dma_start(out=ms_raw[0][:], in_=ms_view[:, :, 0:BANK])
        nc.sync.dma_start(out=ms_raw[1][:], in_=ms_view[:, :, BANK:M])
        nc.sync.dma_start(out=earl_rows[1][:], in_=earl[P:Q, :])
        nc.sync.dma_start(idx3[:], offs3)
        for t in range(PACK):
            nc.sync.dma_start(out=val_rows[t][:], in_=vals_view[t])

        keys = sb.tile([P, I], U16, name="keys", align_bytes=64)
        key_scales = sb.tile([P, I], U8, name="key_scales", align_bytes=64)
        nc.vector.tensor_copy(out=keys[:], in_=key_pool[:].indirect(idx[:]))
        nc.vector.tensor_copy(out=key_scales[:], in_=key_pool_scales[:].indirect(idx[:]))

        q_bf = sb.tile([P, Q, PACK], BF16, name="q_bf", align_bytes=64)
        interleave(nc.scalar.copy, q_bf[:], q_raw[:])
        q_codes, q_scales = quantise("q", q_bf[:].rearrange("p c t -> p (c t)"), Q)
        earl_g = [sb.tile([P, I], F32, name=f"earl_g{h}") for h in range(2)]
        nc.scalar.activation(out=earl_g[0][:], in_=earl_rows[0][:].indirect(idx2[:]), func=COPY)

        w_codes = sb.tile([P, Q], U32, name="w_codes", align_bytes=64)
        w_scales = sb.tile([P, Q], U8, name="w_scales", align_bytes=64)
        scores = []
        for h in range(2):
            q_rows = slice(h * P, (h + 1) * P)
            scores.append(sc.tile([P, BANK], F32, name="score"))
            nc.tensor.matmul_mx(
                out=scores[h][:], lhsT=q_codes[:, q_rows].bitcast(FP8X4), lhsT_scale=q_scales[:, q_rows],
                rhs=keys[:].bitcast(FP4X4), rhs_scale=key_scales[:], start=True, stop=True,
            )

        def weigh(h):
            w = sb.tile([P, I], F32, name=f"w{h}")
            nc.vector.tensor_tensor(out=w[:], in0=scores[h][:], in1=earl_g[h][:], op=MULT)
            return w

        def turn_weights(h, w, w_bf):
            turned = tr.tile([P, PACK, P], F32, name="turned")
            for t in range(PACK):
                nc.tensor.transpose(turned[:, t, :], w[:, t:I:PACK], ident[:])
            nc.vector.tensor_tensor(
                out=w_bf[:], in0=turned[:].rearrange("p t q -> p q t"),
                in1=factor[:].to_broadcast([P, P, PACK]), op=MULT,
            )
            q_rows = slice(h * P, (h + 1) * P)
            nc.vector.quantize_mx(
                out=w_codes[:, q_rows].bitcast(FP8X4), scales=w_scales[:, q_rows],
                in_=w_bf[:].rearrange("p c t -> p (c t)"),
            )

        turn_weights(0, weigh(0), sb.tile([P, P, PACK], BF16, name="w_bf0", align_bytes=64))

        wm_bf = sb.tile([P, PACK * E], BF16, name="wm_bf", align_bytes=64)
        wm_dst = wm_bf[:].rearrange("p (t m j) -> p m t j", t=PACK, j=PACK)
        wm_src = wm_raw[:].rearrange("p j (m t) -> p m t j", t=PACK)
        nc.vector.tensor_copy(out=wm_dst[:, 0:WM_ON_VECTOR], in_=wm_src[:, 0:WM_ON_VECTOR])
        nc.scalar.copy(out=wm_dst[:, WM_ON_VECTOR:P], in_=wm_src[:, WM_ON_VECTOR:P])
        wm_codes, wm_scales = quantise("wm", wm_bf[:], E)
        me = [sb.tile([P, M], F32, name=f"me{t}") for t in range(PACK)]

        def quantise_store(h):
            share = STORE_ON_VECTOR[h]
            ms_bf = sb.tile([P, BANK, PACK], BF16, name=f"ms_bf{h}", align_bytes=64)
            interleave(nc.vector.tensor_copy, ms_bf[:, 0:share, :], ms_raw[h][:, :, 0:share])
            interleave(nc.scalar.copy, ms_bf[:, share:BANK, :], ms_raw[h][:, :, share:BANK])
            return quantise(f"ms{h}", ms_bf[:].rearrange("p c t -> p (c t)"), BANK)

        def memories(h, ms_codes, ms_scales):
            for t in range(PACK):
                features = slice(t * P, (t + 1) * P)
                acc = mm.tile([P, BANK], F32, name="acc")
                nc.tensor.matmul_mx(
                    out=acc[:], lhsT=wm_codes[:, features].bitcast(FP8X4), lhsT_scale=wm_scales[:, features],
                    rhs=ms_codes[:].bitcast(FP8X4), rhs_scale=ms_scales[:], start=True, stop=True,
                )
                nc.scalar.copy(out=me[t][:, h * BANK : (h + 1) * BANK], in_=acc[:])

        store_halves = [quantise_store(h) for h in range(2)]
        for h in range(2):
            memories(h, *store_halves[h])

        nc.vector.tensor_copy(out=earl_g[1][:], in_=earl_rows[1][:].indirect(idx2[:]))
        w1 = weigh(1)
        val_g = [sb.tile([P, I], BF16, name=f"val_g{t}", tag=f"val_g{t}") for t in range(2)]
        nc.vector.tensor_copy(out=val_g[0][:], in_=val_rows[0][:].indirect(idx[:]))
        turn_weights(1, w1, late.tile([P, P, PACK], BF16, name="w_bf1", offset=ON_FIRST_VALUES, align_bytes=64))

        me_g = late.tile(
            [P, LAST, Q], F32, name="me_g", offset=ON_FIRST_VALUES + GROUPED_BYTES, align_bytes=64
        )
        for t in range(LAST):
            nc.vector.tensor_copy(out=me_g[:, t, :], in_=me[t][:].indirect(idx3[:]))

        y = late.tile([P, PACK, Q], F32, name="y", offset=ON_LAST_VALUES, align_bytes=64)
        out_rows = out_0.rearrange("(p t) q -> p t q", t=PACK)

        def turn_values(t, turned):
            pairs = val_g[t][:].bitcast(F32)
            for u in range(2):
                nc.tensor.transpose(turned[:, u, :], pairs[:, u : I // 2 : 2], ident[:])

        def value_product(out, codes, scales):
            nc.tensor.matmul_mx(
                out=out, lhsT=codes.bitcast(FP8X4), lhsT_scale=scales,
                rhs=w_codes[:].bitcast(FP8X4), rhs_scale=w_scales[:], start=True, stop=True,
            )

        def scale_and_store(tiles, sums, memory):
            nc.vector.tensor_tensor(out=y[:, tiles, :], in0=sums[:], in1=memory, op=MULT)
            nc.sync.dma_start(out=out_rows[:, tiles, :], in_=y[:, tiles, :])

        turned_pair = mm.tile([P, 2, 2, P], F32, name="acc")
        nc.scalar.activation(out=val_g[1][:], in_=val_rows[1][:].indirect(idx[:]), func=COPY)
        me_g_last = sb.tile([P, 1, Q], F32, name="me_g_last", tag="val_rows1", align_bytes=64)
        nc.scalar.activation(out=me_g_last[:, 0, :], in_=me[LAST][:].indirect(idx3[:]), func=COPY)
        for t in range(2):
            turn_values(t, turned_pair[:, t])
        pair_bf = sb.tile([P, 2 * P * PACK], BF16, name="v_bf01", align_bytes=64)
        nc.scalar.copy(
            out=pair_bf[:].bitcast(F32).rearrange("p (t e u) -> p t e u", t=2, u=2),
            in_=turned_pair[:].rearrange("p t u e -> p t e u"),
        )
        pair_codes, pair_scales = quantise("v01", pair_bf[:], 2 * P)
        pair_sums = sc.tile([P, 2, Q], F32, name="score")
        for t in range(2):
            features = slice(t * P, (t + 1) * P)
            value_product(pair_sums[:, t, :], pair_codes[:, features], pair_scales[:, features])

        val_g.append(sb.tile([P, I], BF16, name="val_g2", tag="val_g1"))
        val_g.append(sb.tile([P, I], BF16, name="val_g3"))
        half, half_columns = I // 2, I // 2 // STRIPE
        nc.scalar.activation(out=val_g[2][:], in_=val_rows[2][:].indirect(idx[:]), func=COPY)
        nc.vector.tensor_copy(
            out=val_g[LAST][:, 0:half], in_=val_rows[LAST][:].indirect(idx[:, 0:half_columns])
        )
        nc.scalar.activation(
            out=val_g[LAST][:, half:I], in_=val_rows[LAST][:].indirect(idx[:, half_columns : I // STRIPE]),
            func=COPY,
        )
        scale_and_store(slice(0, 2), pair_sums, me_g[:, 0:2, :])

        single_sums = []
        for t in range(2, PACK):
            turned = tr.tile([P, 2, P], F32, name="turned")
            turn_values(t, turned)
            v_bf = late.tile(
                [P, P * PACK], BF16, name=f"v_bf{t}",
                offset=ON_LAST_VALUES + Y_BYTES + GROUPED_BYTES * (t - 2), align_bytes=64,
            )
            nc.scalar.copy(
                out=v_bf[:].bitcast(F32).rearrange("p (e u) -> p e u", u=2),
                in_=turned[:].rearrange("p u e -> p e u"),
            )
            v_codes, v_scales = quantise(f"v{t}", v_bf[:], P)
            sums = mm.tile([P, 1, Q], F32, name="acc")
            value_product(sums[:, 0, :], v_codes[:], v_scales[:])
            single_sums.append(sums)
        scale_and_store(slice(2, LAST), single_sums[0], me_g[:, 2:LAST, :])
        scale_and_store(slice(LAST, PACK), single_sums[1], me_g_last[:])

        y_bf = sb.tile([P, Q, PACK], BF16, name="y_bf", align_bytes=64)
        interleave(nc.vector.tensor_copy, y_bf[:, 0:Y_ON_VECTOR, :], y[:, :, 0:Y_ON_VECTOR])
        interleave(nc.scalar.copy, y_bf[:, Y_ON_VECTOR:Q, :], y[:, :, Y_ON_VECTOR:Q])
        y_codes, y_scales = quantise("y", y_bf[:].rearrange("p c t -> p (c t)"), Q)
        nc.sync.dma_start(
            out=out_1[0].rearrange("p c r -> p (c r)").bitcast(I32), in_=y_codes[:].bitcast(I32)
        )
        for g in range(P // QUADRANT):
            queue = nc.scalar if g % 2 == 0 else nc.sync
            queue.dma_start(
                out=out_2[0, PACK * g : PACK * (g + 1), :].bitcast(I32),
                in_=y_scales[QUADRANT * g : QUADRANT * g + PACK, :].bitcast(I32),
            )
